import numpy as np
import ml_dtypes


def mxq(x, axis, fmt="e4m3"):
    dtype, down = {"e4m3": (ml_dtypes.float8_e4m3fn, 7), "e5m2": (ml_dtypes.float8_e5m2, 14)}[fmt]
    v = np.moveaxis(np.asarray(x, np.float32).astype(ml_dtypes.bfloat16).astype(np.float64), axis, -1)
    blocks = v.reshape(v.shape[:-1] + (-1, 32))
    amax = np.abs(blocks).max(-1, keepdims=True)
    byte = np.maximum(np.where(amax > 0, np.frexp(amax)[1] - 1 + 127, 0) - down, 1)
    scale = np.exp2(byte - 127.0)
    codes = (blocks / scale).astype(np.float32).astype(dtype).astype(np.float64)
    return np.moveaxis((codes * scale).reshape(v.shape), -1, axis)


WIDE = False


def mx_kscale(k):
    if not WIDE:
        return np.ones(k)
    levels = np.array([30, -30])
    if k % 512:
        return np.exp2(np.random.permutation(np.resize(levels, k // 32))).repeat(32)
    a = np.empty((k // 512, 16))
    for p in range(k // 512):
        a[p, :8] = np.random.permutation(np.resize(levels, 8))
        for g in range(8):
            far = levels[np.abs(levels - a[p, g]) >= 10]
            a[p, g + 8] = far[np.random.randint(len(far))]
    return np.exp2(a.ravel()).repeat(32)


def f64(x):
    return np.asarray(x).astype(np.float64)


def striped(idx):
    return np.tile(np.asarray(idx).reshape(-1, 16).T, (8, 1)).astype(np.uint16)


def unstriped(offs):
    return offs[:16].T.reshape(-1).astype(np.int64)


E2M1 = np.array([0.0, 0.5, 1.0, 1.5, 2.0, 3.0, 4.0, 6.0, -0.0, -0.5, -1.0, -1.5, -2.0, -3.0, -4.0, -6.0])


def pack_weight(w, fmt):
    k, n = w.shape
    w = f64(np.asarray(w, np.float32).astype(ml_dtypes.bfloat16)).reshape(k // 32, 32, n)
    amax = np.abs(w).max(1)
    if fmt in ("e4m3", "e5m2"):
        byte = np.frexp(amax)[1] - 1 + 127 - (7 if fmt == "e4m3" else 14)
    else:
        mant, ex = np.frexp(amax / 6.0)
        byte = np.where(mant > 0.5, ex, ex - 1) + 127
    byte = np.clip(np.where(amax > 0, byte, 1), 1, 254)
    scaled = (w * np.exp2(127.0 - byte)[:, None, :]).reshape(k, n).astype(np.float32)
    by_word = np.ascontiguousarray(scaled.reshape(k // 512, 128, 4, n).transpose(0, 1, 3, 2))
    if fmt in ("e4m3", "e5m2"):
        words = by_word.astype(ml_dtypes.float8_e4m3fn if fmt == "e4m3" else ml_dtypes.float8_e5m2).view(np.uint8)
    else:
        c = by_word.astype(ml_dtypes.float4_e2m1fn).view(np.uint8) & 0xF
        words = (c[..., 0::2] | (c[..., 1::2] << 4)).reshape(k // 512, 128, 2 * n)
    return np.ascontiguousarray(words), np.ascontiguousarray(byte.astype(np.uint8).reshape(k // 512, 16, n))


def unpack_weight(words, scales, fmt):
    g, _, n = scales.shape
    words = np.ascontiguousarray(words).reshape(g, 128, n, -1)
    if fmt in ("e4m3", "e5m2"):
        vals = words.view(ml_dtypes.float8_e4m3fn if fmt == "e4m3" else ml_dtypes.float8_e5m2).astype(np.float64)
    else:
        nib = np.empty((g, 128, n, 4), np.uint8)
        nib[..., 0::2] = words & 0xF
        nib[..., 1::2] = words >> 4
        vals = E2M1[nib]
    vals = vals * np.repeat(np.exp2(scales.astype(np.float64) - 127.0), 8, axis=1)[..., None]
    return vals.transpose(0, 1, 3, 2).reshape(g * 512, n)


K, T, J, I, L, S, R, V, N = 512, 1024, 256, 128, 128, 512, 512, 512, 256


def setup_inputs():
    n = np.random.standard_normal
    idx = np.random.permutation(T)[:I]
    idx2 = np.random.permutation(S)[:L]
    idx3 = np.random.permutation(V)[:J]
    fk = mx_kscale(K)
    fr = mx_kscale(R)
    wp = pack_weight(n((K, R)) * 1 / np.sqrt(K) * fk[:, None] * fr, "e2m1")
    wbp = pack_weight(n((R, N)) * 1 / np.sqrt(R) / fr[:, None], "e5m2")
    return {
        "xa": (n((K, T)) / fk[:, None]).astype(np.float32),
        "xb": (n((K, S)) * 0.6 / fk[:, None]).astype(np.float32),
        "w_words": wp[0],
        "w_scales": wp[1],
        "tb": (n((R, V)) * 0.7 * fr[:, None]).astype(np.float32),
        "wb_words": wbp[0],
        "wb_scales": wbp[1],
        "rs": (n((N, J))).astype(np.float32),
        "gm": (np.random.uniform(0.5, 2.0, (N, 1))).astype(np.float32),
        "offs": striped(idx),
        "offs2": striped(idx2),
        "offs3": striped(idx3),
    }


def reference(xa, xb, w_words, w_scales, tb, wb_words, wb_scales, rs, gm, offs, offs2, offs3):
    idx = unstriped(offs)
    idx2 = unstriped(offs2)
    idx3 = unstriped(offs3)
    wu = unpack_weight(w_words, w_scales, "e2m1")
    wbu = unpack_weight(wb_words, wb_scales, "e5m2")
    u = np.concatenate([f64(xa)[:, idx], f64(xb)[:, idx2]], axis=1)
    uq = mxq(u, 0, "e4m3")
    a = wu.T @ uq
    hid = np.maximum(a - f64(tb)[:, idx3], 0.0)
    hidq = mxq(hid, 0, "e5m2")
    p = wbu.T @ hidq
    y = f64(gm) * p + f64(rs)
    return y

@@ -1,0 +1,166 @@
+from contextlib import ExitStack
+
+import concourse.mybir as mybir
+
+K, T, S, R, V, N, J = 512, 1024, 512, 512, 512, 256, 256
+FLOPS = 2 * K * R * J + 2 * R * N * J
+
+F32 = mybir.dt.float32
+BF16 = mybir.dt.bfloat16
+I32 = mybir.dt.int32
+U32 = mybir.dt.uint32
+U16 = mybir.dt.uint16
+U8 = mybir.dt.uint8
+E4M3 = mybir.dt.float8_e4m3fn_x4
+E5M2 = mybir.dt.float8_e5m2_x4
+E2M1 = mybir.dt.float4_e2m1fn_x4
+ALU = mybir.AluOpType
+ACT = mybir.ActivationFunctionType
+
+P = 128
+PACK = 4
+H = 128
+
+
+def tile_list_joined_overtable_residual_kernel(
+    tc, xa, xb, w_words, w_scales, tb, wb_words, wb_scales, rs, gm, offs, offs2, offs3, out
+):
+    nc = tc.nc
+    with ExitStack() as ctx:
+        sb = ctx.enter_context(tc.tile_pool(name="sb", bufs=1))
+        ps = ctx.enter_context(tc.psum_pool(name="ps", bufs=1))
+
+        def tile(name, shape, dtype):
+            return sb.tile(shape, dtype, name=name, align_bytes=64)
+
+        xa_p = xa.rearrange("(p t) c -> p t c", t=PACK)
+        xb_p = xb.rearrange("(p t) c -> p t c", t=PACK)
+        tb_p = tb.rearrange("(p t) c -> p t c", t=PACK)
+
+        la = sb.tile([P, 8], U16, name="la")
+        lb = sb.tile([P, 8], U16, name="lb")
+        lt = sb.tile([P, 16], U16, name="lt")
+        w_raw = tile("w_raw", [P, R], U16)
+        sc = tile("sc", [P, R + N], U8)
+        ws_raw = sc[:, 0:R]
+        wb_c = tile("wb_c", [P, N], U32)
+        wb_s = sc[:, R : R + N]
+        gm_sb = tile("gm_sb", [P, 2], F32)
+        rs_sb = tile("rs_sb", [P, 2, J], F32)
+        xb_sb = tile("xb_sb", [P, PACK, S], F32)
+        xa01 = tile("xa01", [P, 2, T], F32)
+        xa2 = tile("xa2", [P, T], F32)
+        xa3 = tile("xa3", [P, T], F32)
+        tb_sb = [tile(f"tb{t}", [P, V], F32) for t in range(PACK)]
+
+        nc.vector.memset(sc[:].bitcast(I32), 0)
+        nc.sync.dma_start(xb_sb[:], xb_p)
+        nc.sync.dma_start(lb[:], offs2)
+        nc.sync.dma_start(w_raw[:].bitcast(I32), w_words[0].bitcast(I32))
+        for q in range(4):
+            nc.sync.dma_start(ws_raw[32 * q : 32 * q + 4, :].bitcast(I32), w_scales[0, 4 * q : 4 * q + 4, :].bitcast(I32))
+        nc.sync.dma_start(xa01[:], xa_p[:, 0:2, :])
+        nc.sync.dma_start(la[:], offs)
+        nc.sync.dma_start(xa2[:], xa_p[:, 2, :])
+        nc.sync.dma_start(xa3[:], xa_p[:, 3, :])
+        nc.sync.dma_start(lt[:], offs3)
+        for t in range(PACK):
+            nc.sync.dma_start(tb_sb[t][:], tb_p[:, t, :])
+        nc.sync.dma_start(wb_c[:].bitcast(I32), wb_words[0].rearrange("p n t -> p (n t)").bitcast(I32))
+        nc.sync.dma_start(rs_sb[:], rs.rearrange("(c p) j -> p c j", p=P))
+        for q in range(4):
+            nc.gpsimd.dma_start(wb_s[32 * q : 32 * q + 4, :].bitcast(I32), wb_scales[0, 4 * q : 4 * q + 4, :].bitcast(I32))
+        with nc.allow_non_contiguous_dma(reason="one factor a partition"):
+            nc.gpsimd.dma_start(gm_sb[:], gm.rearrange("(c p) o -> p (c o)", p=P))
+
+        w_c = tile("w_c", [P, R], U16)
+        w_s = tile("w_s", [P, R], U8)
+        nc.vector.tensor_copy(w_c[:].rearrange("p (t m) -> p t m", t=PACK), w_raw[:].rearrange("p (m t) -> p t m", t=PACK))
+        nc.vector.tensor_copy(w_s[:].rearrange("p (t m) -> p t m", t=PACK), ws_raw.rearrange("p (m t) -> p t m", t=PACK))
+
+        a_b = ps.tile([P, PACK, H], F32, name="a_b")
+        a_a = [ps.tile([P, 2, H], F32, name=f"a_a{u}") for u in range(2)]
+        p_ps = [ps.tile([P, 2, H], F32, name=f"p{h}") for h in range(2)]
+
+        def quantise(name, src, fmt):
+            codes = tile(name + "_c", [P, H], U32)
+            scales = tile(name + "_s", [P, H], U8)
+            nc.vector.quantize_mx(out=codes[:].bitcast(fmt), scales=scales[:], in_=src[:].rearrange("p j t -> p (j t)"))
+            return codes, scales
+
+        def first_product(sums, codes, scales):
+            for t in range(PACK):
+                nc.tensor.matmul_mx(
+                    out=sums[t],
+                    lhsT=w_c[:, t * P : (t + 1) * P].bitcast(E2M1),
+                    lhsT_scale=w_s[:, t * P : (t + 1) * P],
+                    rhs=codes[:].bitcast(E4M3),
+                    rhs_scale=scales[:],
+                    start=True,
+                    stop=True,
+                )
+
+        def woven(dst, src):
+            return (
+                dst.rearrange("p (c i) t -> p c t i", i=4),
+                src.rearrange("p t (c i) -> p c t i", i=4),
+            )
+
+        gb = tile("gb", [P, PACK, H], F32)
+        for t in range(PACK):
+            nc.scalar.activation(gb[:, t, :], xb_sb[:, t, :].indirect(lb[:]), ACT.Copy)
+        ub = tile("ub", [P, H, PACK], BF16)
+        nc.scalar.copy(*woven(ub[:], gb[:]))
+        first_product([a_b[:, t, :] for t in range(PACK)], *quantise("ub", ub, E4M3))
+
+        ua = tile("ua", [P, H, PACK], BF16)
+        for t, window in enumerate((xa01[:, 0, :], xa01[:, 1, :], xa2[:], xa3[:])):
+            nc.vector.tensor_copy(ua[:, :, t], window.indirect(la[:]))
+        first_product([a_a[t // 2][:, t % 2, :] for t in range(PACK)], *quantise("ua", ua, E4M3))
+
+        da = tile("da", [P, PACK, H], BF16)
+        db = tile("db", [P, PACK, H], BF16)
+        g01 = tile("g01", [P, 2, J], F32)
+        g2 = tile("g2", [P, J], F32)
+        g3a = tile("g3a", [P, H], F32)
+        g3b = tile("g3b", [P, H], F32)
+        for t in range(2):
+            nc.scalar.activation(g01[:, t, :], tb_sb[t][:].indirect(lt[:]), ACT.Copy)
+            nc.vector.tensor_tensor(db[:, t, :], a_b[:, t, :], g01[:, t, H:J], ALU.subtract)
+        nc.vector.tensor_tensor(da[:, 0:2, :], a_a[0][:], g01[:, :, 0:H], ALU.subtract)
+        nc.scalar.activation(g2[:], tb_sb[2][:].indirect(lt[:]), ACT.Copy)
+        nc.vector.tensor_tensor(da[:, 2, :], a_a[1][:, 0, :], g2[:, 0:H], ALU.subtract)
+        nc.vector.tensor_tensor(db[:, 2, :], a_b[:, 2, :], g2[:, H:J], ALU.subtract)
+        nc.vector.tensor_copy(g3a[:], tb_sb[3][:].indirect(lt[:, 0:8]))
+        nc.scalar.activation(g3b[:], tb_sb[3][:].indirect(lt[:, 8:16]), ACT.Copy)
+        nc.vector.tensor_tensor(da[:, 3, :], a_a[1][:, 1, :], g3a[:], ALU.subtract)
+        nc.vector.tensor_tensor(db[:, 3, :], a_b[:, 3, :], g3b[:], ALU.subtract)
+
+        hid = [tile(f"hid{h}", [P, H, PACK], BF16) for h in range(2)]
+        dst, src = woven(hid[0][:], da[:])
+        nc.vector.tensor_scalar(dst, src, 0.0, None, ALU.max)
+        dst, src = woven(hid[1][:, 0:64, :], db[:, :, 0:64])
+        nc.scalar.activation(dst, src, ACT.Relu)
+        dst, src = woven(hid[1][:, 64:H, :], db[:, :, 64:H])
+        nc.vector.tensor_scalar(dst, src, 0.0, None, ALU.max)
+
+        hq = [quantise(f"hq{h}", hid[h], E5M2) for h in range(2)]
+        out_p = out.rearrange("(c p) j -> p c j", p=P)
+        for h in range(2):
+            for c in range(2):
+                nc.tensor.matmul_mx(
+                    out=p_ps[h][:, c, :],
+                    lhsT=wb_c[:, c * P : (c + 1) * P].bitcast(E5M2),
+                    lhsT_scale=wb_s[:, c * P : (c + 1) * P],
+                    rhs=hq[h][0][:].bitcast(E5M2),
+                    rhs_scale=hq[h][1][:],
+                    start=True,
+                    stop=True,
+                )
+        for h in range(2):
+            y = tile(f"y{h}", [P, 2, H], F32)
+            for c in range(2):
+                nc.vector.scalar_tensor_tensor(
+                    y[:, c, :], p_ps[h][:, c, :], gm_sb[:, c : c + 1], rs_sb[:, c, h * H : (h + 1) * H], ALU.mult, ALU.add
+                )
+            nc.sync.dma_start(out_p[:, :, h * H : (h + 1) * H], y[:])

@@ -67,11 +67,11 @@ def tile_list_joined_overtable_residual_kernel(
         for t in range(PACK):
             nc.sync.dma_start(tb_sb[t][:], tb_p[:, t, :])
         nc.sync.dma_start(wb_c[:].bitcast(I32), wb_words[0].rearrange("p n t -> p (n t)").bitcast(I32))
-        nc.sync.dma_start(rs_sb[:], rs.rearrange("(c p) j -> p c j", p=P))
-        for q in range(4):
-            nc.gpsimd.dma_start(wb_s[32 * q : 32 * q + 4, :].bitcast(I32), wb_scales[0, 4 * q : 4 * q + 4, :].bitcast(I32))
         with nc.allow_non_contiguous_dma(reason="one factor a partition"):
-            nc.gpsimd.dma_start(gm_sb[:], gm.rearrange("(c p) o -> p (c o)", p=P))
+            nc.sync.dma_start(gm_sb[:], gm.rearrange("(c p) o -> p (c o)", p=P))
+        for q in range(4):
+            nc.sync.dma_start(wb_s[32 * q : 32 * q + 4, :].bitcast(I32), wb_scales[0, 4 * q : 4 * q + 4, :].bitcast(I32))
+        nc.sync.dma_start(rs_sb[:], rs.rearrange("(c p) j -> p c j", p=P))
 
         w_c = tile("w_c", [P, R], U16)
         w_s = tile("w_s", [P, R], U8)
@@ -80,7 +80,6 @@ def tile_list_joined_overtable_residual_kernel(
 
         a_b = ps.tile([P, PACK, H], F32, name="a_b")
         a_a = [ps.tile([P, 2, H], F32, name=f"a_a{u}") for u in range(2)]
-        p_ps = [ps.tile([P, 2, H], F32, name=f"p{h}") for h in range(2)]
 
         def quantise(name, src, fmt):
             codes = tile(name + "_c", [P, H], U32)
@@ -148,8 +147,10 @@ def tile_list_joined_overtable_residual_kernel(
         out_p = out.rearrange("(c p) j -> p c j", p=P)
         for h in range(2):
             for c in range(2):
+                y = tile(f"y{h}{c}", [P, H], F32)
+                p_ps = ps.tile([P, H], F32, name=f"p{h}{c}")
                 nc.tensor.matmul_mx(
-                    out=p_ps[h][:, c, :],
+                    out=p_ps[:],
                     lhsT=wb_c[:, c * P : (c + 1) * P].bitcast(E5M2),
                     lhsT_scale=wb_s[:, c * P : (c + 1) * P],
                     rhs=hq[h][0][:].bitcast(E5M2),
@@ -157,10 +158,7 @@ def tile_list_joined_overtable_residual_kernel(
                     start=True,
                     stop=True,
                 )
-        for h in range(2):
-            y = tile(f"y{h}", [P, 2, H], F32)
-            for c in range(2):
                 nc.vector.scalar_tensor_tensor(
-                    y[:, c, :], p_ps[h][:, c, :], gm_sb[:, c : c + 1], rs_sb[:, c, h * H : (h + 1) * H], ALU.mult, ALU.add
+                    y[:], p_ps[:], gm_sb[:, c : c + 1], rs_sb[:, c, h * H : (h + 1) * H], ALU.mult, ALU.add
                 )
-            nc.sync.dma_start(out_p[:, :, h * H : (h + 1) * H], y[:])
+                (nc.scalar, nc.sync)[c].dma_start(out_p[:, c, h * H : (h + 1) * H], y[:])

@@ -79,7 +79,7 @@ def tile_list_joined_overtable_residual_kernel(
         nc.vector.tensor_copy(w_s[:].rearrange("p (t m) -> p t m", t=PACK), ws_raw.rearrange("p (m t) -> p t m", t=PACK))
 
         a_b = ps.tile([P, PACK, H], F32, name="a_b")
-        a_a = [ps.tile([P, 2, H], F32, name=f"a_a{u}") for u in range(2)]
+        a_a = ps.tile([P, PACK, H], F32, name="a_a")
 
         def quantise(name, src, fmt):
             codes = tile(name + "_c", [P, H], U32)
@@ -105,47 +105,35 @@ def tile_list_joined_overtable_residual_kernel(
                 src.rearrange("p t (c i) -> p c t i", i=4),
             )
 
-        gb = tile("gb", [P, PACK, H], F32)
-        for t in range(PACK):
-            nc.scalar.activation(gb[:, t, :], xb_sb[:, t, :].indirect(lb[:]), ACT.Copy)
         ub = tile("ub", [P, H, PACK], BF16)
-        nc.scalar.copy(*woven(ub[:], gb[:]))
+        for t in range(PACK):
+            nc.vector.tensor_copy(ub[:, :, t], xb_sb[:, t, :].indirect(lb[:]))
         first_product([a_b[:, t, :] for t in range(PACK)], *quantise("ub", ub, E4M3))
+        ab_sb = tile("ab_sb", [P, PACK, H], F32)
+        nc.scalar.activation(ab_sb[:], a_b[:], ACT.Copy)
 
         ua = tile("ua", [P, H, PACK], BF16)
         for t, window in enumerate((xa01[:, 0, :], xa01[:, 1, :], xa2[:], xa3[:])):
             nc.vector.tensor_copy(ua[:, :, t], window.indirect(la[:]))
-        first_product([a_a[t // 2][:, t % 2, :] for t in range(PACK)], *quantise("ua", ua, E4M3))
+        first_product([a_a[:, t, :] for t in range(PACK)], *quantise("ua", ua, E4M3))
 
-        da = tile("da", [P, PACK, H], BF16)
-        db = tile("db", [P, PACK, H], BF16)
-        g01 = tile("g01", [P, 2, J], F32)
-        g2 = tile("g2", [P, J], F32)
-        g3a = tile("g3a", [P, H], F32)
-        g3b = tile("g3b", [P, H], F32)
-        for t in range(2):
-            nc.scalar.activation(g01[:, t, :], tb_sb[t][:].indirect(lt[:]), ACT.Copy)
-            nc.vector.tensor_tensor(db[:, t, :], a_b[:, t, :], g01[:, t, H:J], ALU.subtract)
-        nc.vector.tensor_tensor(da[:, 0:2, :], a_a[0][:], g01[:, :, 0:H], ALU.subtract)
-        nc.scalar.activation(g2[:], tb_sb[2][:].indirect(lt[:]), ACT.Copy)
-        nc.vector.tensor_tensor(da[:, 2, :], a_a[1][:, 0, :], g2[:, 0:H], ALU.subtract)
-        nc.vector.tensor_tensor(db[:, 2, :], a_b[:, 2, :], g2[:, H:J], ALU.subtract)
-        nc.vector.tensor_copy(g3a[:], tb_sb[3][:].indirect(lt[:, 0:8]))
-        nc.scalar.activation(g3b[:], tb_sb[3][:].indirect(lt[:, 8:16]), ACT.Copy)
-        nc.vector.tensor_tensor(da[:, 3, :], a_a[1][:, 1, :], g3a[:], ALU.subtract)
-        nc.vector.tensor_tensor(db[:, 3, :], a_b[:, 3, :], g3b[:], ALU.subtract)
+        da = tile("da", [P, H, PACK], BF16)
+        db = tile("db", [P, PACK, H], F32)
+        ga = tile("ga", [P, PACK, H], F32)
+        for t in range(PACK):
+            nc.scalar.activation(ga[:, t, :], tb_sb[t][:].indirect(lt[:, 0:8]), ACT.Copy)
+            nc.vector.tensor_tensor(db[:, t, :], tb_sb[t][:].indirect(lt[:, 8:16]), ab_sb[:, t, :], ALU.subtract)
 
         hid = [tile(f"hid{h}", [P, H, PACK], BF16) for h in range(2)]
-        dst, src = woven(hid[0][:], da[:])
-        nc.vector.tensor_scalar(dst, src, 0.0, None, ALU.max)
-        dst, src = woven(hid[1][:, 0:64, :], db[:, :, 0:64])
-        nc.scalar.activation(dst, src, ACT.Relu)
-        dst, src = woven(hid[1][:, 64:H, :], db[:, :, 64:H])
-        nc.vector.tensor_scalar(dst, src, 0.0, None, ALU.max)
+        dst, src = woven(hid[1][:], db[:])
+        nc.scalar.activation(dst, src, ACT.Relu, scale=-1.0)
+        dst, src = woven(da[:], a_a[:])
+        nc.vector.tensor_tensor(dst, src, woven(da[:], ga[:])[1], ALU.subtract)
+        nc.vector.tensor_scalar(hid[0][:], da[:], 0.0, None, ALU.max)
 
-        hq = [quantise(f"hq{h}", hid[h], E5M2) for h in range(2)]
+        hq = {h: quantise(f"hq{h}", hid[h], E5M2) for h in (1, 0)}
         out_p = out.rearrange("(c p) j -> p c j", p=P)
-        for h in range(2):
+        for h in (1, 0):
             for c in range(2):
                 y = tile(f"y{h}{c}", [P, H], F32)
                 p_ps = ps.tile([P, H], F32, name=f"p{h}{c}")

@@ -49,8 +49,7 @@ def tile_list_joined_overtable_residual_kernel(
         rs_sb = tile("rs_sb", [P, 2, J], F32)
         xb_sb = tile("xb_sb", [P, PACK, S], F32)
         xa01 = tile("xa01", [P, 2, T], F32)
-        xa2 = tile("xa2", [P, T], F32)
-        xa3 = tile("xa3", [P, T], F32)
+        xa23 = tile("xa23", [P, 2, T], F32)
         tb_sb = [tile(f"tb{t}", [P, V], F32) for t in range(PACK)]
 
         nc.vector.memset(sc[:].bitcast(I32), 0)
@@ -61,9 +60,8 @@ def tile_list_joined_overtable_residual_kernel(
             nc.sync.dma_start(ws_raw[32 * q : 32 * q + 4, :].bitcast(I32), w_scales[0, 4 * q : 4 * q + 4, :].bitcast(I32))
         nc.sync.dma_start(xa01[:], xa_p[:, 0:2, :])
         nc.sync.dma_start(la[:], offs)
-        nc.sync.dma_start(xa2[:], xa_p[:, 2, :])
-        nc.sync.dma_start(xa3[:], xa_p[:, 3, :])
         nc.sync.dma_start(lt[:], offs3)
+        nc.sync.dma_start(xa23[:], xa_p[:, 2:4, :])
         for t in range(PACK):
             nc.sync.dma_start(tb_sb[t][:], tb_p[:, t, :])
         nc.sync.dma_start(wb_c[:].bitcast(I32), wb_words[0].rearrange("p n t -> p (n t)").bitcast(I32))
@@ -113,7 +111,7 @@ def tile_list_joined_overtable_residual_kernel(
         nc.scalar.activation(ab_sb[:], a_b[:], ACT.Copy)
 
         ua = tile("ua", [P, H, PACK], BF16)
-        for t, window in enumerate((xa01[:, 0, :], xa01[:, 1, :], xa2[:], xa3[:])):
+        for t, window in enumerate((xa01[:, 0, :], xa01[:, 1, :], xa23[:, 0, :], xa23[:, 1, :])):
             nc.vector.tensor_copy(ua[:, :, t], window.indirect(la[:]))
         first_product([a_a[:, t, :] for t in range(PACK)], *quantise("ua", ua, E4M3))
 

from contextlib import ExitStack

import concourse.mybir as mybir

K, T, S, R, V, N, J = 512, 1024, 512, 512, 512, 256, 256
FLOPS = 2 * K * R * J + 2 * R * N * J

F32 = mybir.dt.float32
BF16 = mybir.dt.bfloat16
I32 = mybir.dt.int32
U32 = mybir.dt.uint32
U16 = mybir.dt.uint16
U8 = mybir.dt.uint8
E4M3 = mybir.dt.float8_e4m3fn_x4
E5M2 = mybir.dt.float8_e5m2_x4
E2M1 = mybir.dt.float4_e2m1fn_x4
ALU = mybir.AluOpType
ACT = mybir.ActivationFunctionType

P = 128
PACK = 4
H = 128


def tile_list_joined_overtable_residual_kernel(
    tc, xa, xb, w_words, w_scales, tb, wb_words, wb_scales, rs, gm, offs, offs2, offs3, out
):
    nc = tc.nc
    with ExitStack() as ctx:
        sb = ctx.enter_context(tc.tile_pool(name="sb", bufs=1))
        ps = ctx.enter_context(tc.psum_pool(name="ps", bufs=1))

        def tile(name, shape, dtype):
            return sb.tile(shape, dtype, name=name, align_bytes=64)

        xa_p = xa.rearrange("(p t) c -> p t c", t=PACK)
        xb_p = xb.rearrange("(p t) c -> p t c", t=PACK)
        tb_p = tb.rearrange("(p t) c -> p t c", t=PACK)

        la = sb.tile([P, 8], U16, name="la")
        lb = sb.tile([P, 8], U16, name="lb")
        lt = sb.tile([P, 16], U16, name="lt")
        w_raw = tile("w_raw", [P, R], U16)
        sc = tile("sc", [P, R + N], U8)
        ws_raw = sc[:, 0:R]
        wb_c = tile("wb_c", [P, N], U32)
        wb_s = sc[:, R : R + N]
        gm_sb = tile("gm_sb", [P, 2], F32)
        rs_sb = tile("rs_sb", [P, 2, J], F32)
        xb_sb = tile("xb_sb", [P, PACK, S], F32)
        xa01 = tile("xa01", [P, 2, T], F32)
        xa23 = tile("xa23", [P, 2, T], F32)
        tb_sb = [tile(f"tb{t}", [P, V], F32) for t in range(PACK)]

        nc.vector.memset(sc[:].bitcast(I32), 0)
        nc.sync.dma_start(xb_sb[:], xb_p)
        nc.sync.dma_start(lb[:], offs2)
        nc.sync.dma_start(w_raw[:].bitcast(I32), w_words[0].bitcast(I32))
        for q in range(4):
            nc.sync.dma_start(ws_raw[32 * q : 32 * q + 4, :].bitcast(I32), w_scales[0, 4 * q : 4 * q + 4, :].bitcast(I32))
        nc.sync.dma_start(xa01[:], xa_p[:, 0:2, :])
        nc.sync.dma_start(la[:], offs)
        nc.sync.dma_start(lt[:], offs3)
        nc.sync.dma_start(xa23[:], xa_p[:, 2:4, :])
        for t in range(PACK):
            nc.sync.dma_start(tb_sb[t][:], tb_p[:, t, :])
        nc.sync.dma_start(wb_c[:].bitcast(I32), wb_words[0].rearrange("p n t -> p (n t)").bitcast(I32))
        with nc.allow_non_contiguous_dma(reason="one factor a partition"):
            nc.sync.dma_start(gm_sb[:], gm.rearrange("(c p) o -> p (c o)", p=P))
        for q in range(4):
            nc.sync.dma_start(wb_s[32 * q : 32 * q + 4, :].bitcast(I32), wb_scales[0, 4 * q : 4 * q + 4, :].bitcast(I32))
        nc.sync.dma_start(rs_sb[:], rs.rearrange("(c p) j -> p c j", p=P))

        w_c = tile("w_c", [P, R], U16)
        w_s = tile("w_s", [P, R], U8)
        nc.vector.tensor_copy(w_c[:].rearrange("p (t m) -> p t m", t=PACK), w_raw[:].rearrange("p (m t) -> p t m", t=PACK))
        nc.vector.tensor_copy(w_s[:].rearrange("p (t m) -> p t m", t=PACK), ws_raw.rearrange("p (m t) -> p t m", t=PACK))

        a_b = ps.tile([P, PACK, H], F32, name="a_b")
        a_a = ps.tile([P, PACK, H], F32, name="a_a")

        def quantise(name, src, fmt):
            codes = tile(name + "_c", [P, H], U32)
            scales = tile(name + "_s", [P, H], U8)
            nc.vector.quantize_mx(out=codes[:].bitcast(fmt), scales=scales[:], in_=src[:].rearrange("p j t -> p (j t)"))
            return codes, scales

        def first_product(sums, codes, scales):
            for t in range(PACK):
                nc.tensor.matmul_mx(
                    out=sums[t],
                    lhsT=w_c[:, t * P : (t + 1) * P].bitcast(E2M1),
                    lhsT_scale=w_s[:, t * P : (t + 1) * P],
                    rhs=codes[:].bitcast(E4M3),
                    rhs_scale=scales[:],
                    start=True,
                    stop=True,
                )

        def woven(dst, src):
            return (
                dst.rearrange("p (c i) t -> p c t i", i=4),
                src.rearrange("p t (c i) -> p c t i", i=4),
            )

        ub = tile("ub", [P, H, PACK], BF16)
        for t in range(PACK):
            nc.vector.tensor_copy(ub[:, :, t], xb_sb[:, t, :].indirect(lb[:]))
        first_product([a_b[:, t, :] for t in range(PACK)], *quantise("ub", ub, E4M3))
        ab_sb = tile("ab_sb", [P, PACK, H], F32)
        nc.scalar.activation(ab_sb[:], a_b[:], ACT.Copy)

        ua = tile("ua", [P, H, PACK], BF16)
        for t, window in enumerate((xa01[:, 0, :], xa01[:, 1, :], xa23[:, 0, :], xa23[:, 1, :])):
            nc.vector.tensor_copy(ua[:, :, t], window.indirect(la[:]))
        first_product([a_a[:, t, :] for t in range(PACK)], *quantise("ua", ua, E4M3))

        da = tile("da", [P, H, PACK], BF16)
        db = tile("db", [P, PACK, H], F32)
        ga = tile("ga", [P, PACK, H], F32)
        for t in range(PACK):
            nc.scalar.activation(ga[:, t, :], tb_sb[t][:].indirect(lt[:, 0:8]), ACT.Copy)
            nc.vector.tensor_tensor(db[:, t, :], tb_sb[t][:].indirect(lt[:, 8:16]), ab_sb[:, t, :], ALU.subtract)

        hid = [tile(f"hid{h}", [P, H, PACK], BF16) for h in range(2)]
        dst, src = woven(hid[1][:], db[:])
        nc.scalar.activation(dst, src, ACT.Relu, scale=-1.0)
        dst, src = woven(da[:], a_a[:])
        nc.vector.tensor_tensor(dst, src, woven(da[:], ga[:])[1], ALU.subtract)
        nc.vector.tensor_scalar(hid[0][:], da[:], 0.0, None, ALU.max)

        hq = {h: quantise(f"hq{h}", hid[h], E5M2) for h in (1, 0)}
        out_p = out.rearrange("(c p) j -> p c j", p=P)
        for h in (1, 0):
            for c in range(2):
                y = tile(f"y{h}{c}", [P, H], F32)
                p_ps = ps.tile([P, H], F32, name=f"p{h}{c}")
                nc.tensor.matmul_mx(
                    out=p_ps[:],
                    lhsT=wb_c[:, c * P : (c + 1) * P].bitcast(E5M2),
                    lhsT_scale=wb_s[:, c * P : (c + 1) * P],
                    rhs=hq[h][0][:].bitcast(E5M2),
                    rhs_scale=hq[h][1][:],
                    start=True,
                    stop=True,
                )
                nc.vector.scalar_tensor_tensor(
                    y[:], p_ps[:], gm_sb[:, c : c + 1], rs_sb[:, c, h * H : (h + 1) * H], ALU.mult, ALU.add
                )
                (nc.scalar, nc.sync)[c].dma_start(out_p[:, c, h * H : (h + 1) * H], y[:])
